import numpy as np
import ml_dtypes

BF16 = ml_dtypes.bfloat16


def bf(x):
    return np.asarray(x, np.float32).astype(BF16)


def f32(x):
    return np.asarray(x, np.float32)


def f64(x):
    return np.asarray(x).astype(np.float64)


def striped(idx):
    return np.tile(idx.reshape(-1, 16).T, (8, 1))


def rows(idx, k):
    return np.tile(idx, (k, 1))


def look(tab, idx):
    return np.take_along_axis(f64(tab), rows(idx, len(tab)), axis=1)


K, S, D, V, N, M = 256, 2048, 3, 512, 1536, 512


def setup_inputs():
    return {"tab": f32(np.random.standard_normal((K, S))), "x0": f32(np.random.standard_normal((K, V))), "w": bf(np.random.standard_normal((K, M)) / np.sqrt(K)), "b": f32(0.5 * np.random.standard_normal((M, 1))), "offs": striped(np.random.permutation(S)[:N])}


def reference(tab, x0, w, b, offs):
    idx = offs[:16].T.reshape(-1)
    x = f64(x0)
    for d in range(D):
        x = np.maximum(x, look(tab, idx[d * V:(d + 1) * V]))
    y = f64(w).T @ x
    return np.maximum(y + f64(b), 0.0)

@@ -1,0 +1,58 @@
+import concourse.mybir as mybir
+
+P = 128
+K, S, D, V, M = 256, 2048, 3, 512, 512
+ROW_BLOCKS = K // P
+OUT_PER_PARTITION = M // P
+LIST_COLUMNS = V // 16
+FLOPS = 2 * K * M * V
+
+F32, BF16, U16 = mybir.dt.float32, mybir.dt.bfloat16, mybir.dt.uint16
+MAX = mybir.AluOpType.max
+RELU = mybir.ActivationFunctionType.Relu
+
+
+def tile_lookup_pool_max_relu_kernel(tc, tab, x0, w, b, offs, out):
+    nc = tc.nc
+    with (
+        tc.tile_pool(name="held", bufs=1) as held,
+        tc.tile_pool(name="running", bufs=2) as running,
+        tc.psum_pool(name="psum", bufs=1) as psum,
+    ):
+        offsets = held.tile([P, D * LIST_COLUMNS], U16, name="offsets")
+        nc.sync.dma_start(offsets[:], offs)
+        windows, centres = [], []
+        for blk in range(ROW_BLOCKS):
+            rows = slice(blk * P, (blk + 1) * P)
+            centre = held.tile([P, V], F32, name=f"centre{blk}")
+            window = held.tile([P, S], F32, name=f"window{blk}")
+            nc.sync.dma_start(centre[:], x0[rows, :])
+            nc.sync.dma_start(window[:], tab[rows, :])
+            windows.append(window)
+            centres.append(centre)
+        weights = held.tile([P, ROW_BLOCKS, M], BF16, name="weights")
+        nc.sync.dma_start(weights[:], w.rearrange("(k p) m -> p k m", p=P))
+        bias = held.tile([P, OUT_PER_PARTITION], F32, name="bias")
+        nc.sync.dma_start(bias[:], b.rearrange("(p c) one -> p (c one)", p=P))
+
+        pooled = []
+        for blk in range(ROW_BLOCKS):
+            best = centres[blk]
+            for d in range(D):
+                piece = offsets[:, d * LIST_COLUMNS : (d + 1) * LIST_COLUMNS]
+                better = running.tile([P, V], F32, name="better")
+                nc.vector.tensor_tensor(better[:], windows[blk][:].indirect(piece), best[:], MAX)
+                best = better
+            rounded = held.tile([P, V], BF16, name=f"rounded{blk}")
+            nc.scalar.copy(rounded[:], best[:])
+            pooled.append(rounded)
+
+        out_rows = out.rearrange("(p c) j -> p c j", p=P)
+        for c in range(OUT_PER_PARTITION):
+            product = psum.tile([P, V], F32, name=f"product{c}")
+            for blk in range(ROW_BLOCKS):
+                nc.tensor.matmul(product[:], weights[:, blk, c::OUT_PER_PARTITION], pooled[blk][:],
+                                 start=blk == 0, stop=blk == ROW_BLOCKS - 1)
+            result = held.tile([P, V], F32, name=f"result{c}")
+            nc.scalar.activation(result[:], product[:], RELU, bias=bias[:, c : c + 1])
+            nc.sync.dma_start(out_rows[:, c, :], result[:])

@@ -4,11 +4,13 @@ P = 128
 K, S, D, V, M = 256, 2048, 3, 512, 512
 ROW_BLOCKS = K // P
 OUT_PER_PARTITION = M // P
-LIST_COLUMNS = V // 16
+ENTRIES_PER_COLUMN = 16
+HALF = V // 2
+CHUNK = 128
 FLOPS = 2 * K * M * V
 
 F32, BF16, U16 = mybir.dt.float32, mybir.dt.bfloat16, mybir.dt.uint16
-MAX = mybir.AluOpType.max
+ADD, MAX = mybir.AluOpType.add, mybir.AluOpType.max
 RELU = mybir.ActivationFunctionType.Relu
 
 
@@ -16,43 +18,54 @@ def tile_lookup_pool_max_relu_kernel(tc, tab, x0, w, b, offs, out):
     nc = tc.nc
     with (
         tc.tile_pool(name="held", bufs=1) as held,
-        tc.tile_pool(name="running", bufs=2) as running,
-        tc.psum_pool(name="psum", bufs=1) as psum,
+        tc.psum_pool(name="psum", bufs=2) as psum,
     ):
-        offsets = held.tile([P, D * LIST_COLUMNS], U16, name="offsets")
-        nc.sync.dma_start(offsets[:], offs)
-        windows, centres = [], []
-        for blk in range(ROW_BLOCKS):
-            rows = slice(blk * P, (blk + 1) * P)
-            centre = held.tile([P, V], F32, name=f"centre{blk}")
-            window = held.tile([P, S], F32, name=f"window{blk}")
-            nc.sync.dma_start(centre[:], x0[rows, :])
-            nc.sync.dma_start(window[:], tab[rows, :])
-            windows.append(window)
-            centres.append(centre)
+        offsets = held.tile([P, D * V // ENTRIES_PER_COLUMN], U16, name="offsets")
+        windows = [held.tile([P, S], F32, name=f"window{blk}") for blk in range(ROW_BLOCKS)]
+        centres = [held.tile([P, V], F32, name=f"centre{blk}") for blk in range(ROW_BLOCKS)]
         weights = held.tile([P, ROW_BLOCKS, M], BF16, name="weights")
-        nc.sync.dma_start(weights[:], w.rearrange("(k p) m -> p k m", p=P))
         bias = held.tile([P, OUT_PER_PARTITION], F32, name="bias")
+        nc.sync.dma_start(offsets[:], offs)
+        nc.sync.dma_start(centres[0][:, :HALF], x0[:P, :HALF])
+        nc.sync.dma_start(windows[0][:], tab[:P, :])
+        nc.sync.dma_start(centres[0][:, HALF:], x0[:P, HALF:])
+        nc.sync.dma_start(windows[1][:], tab[P:, :])
+        nc.sync.dma_start(centres[1][:], x0[P:, :])
+        nc.sync.dma_start(weights[:], w.rearrange("(k p) m -> p k m", p=P))
         nc.sync.dma_start(bias[:], b.rearrange("(p c) one -> p (c one)", p=P))
 
-        pooled = []
-        for blk in range(ROW_BLOCKS):
-            best = centres[blk]
+        def pool_columns(blk, first, width):
+            best = centres[blk][:, first : first + width]
             for d in range(D):
-                piece = offsets[:, d * LIST_COLUMNS : (d + 1) * LIST_COLUMNS]
-                better = running.tile([P, V], F32, name="better")
-                nc.vector.tensor_tensor(better[:], windows[blk][:].indirect(piece), best[:], MAX)
-                best = better
-            rounded = held.tile([P, V], BF16, name=f"rounded{blk}")
-            nc.scalar.copy(rounded[:], best[:])
-            pooled.append(rounded)
+                entry = d * V + first
+                piece = offsets[:, entry // ENTRIES_PER_COLUMN : (entry + width) // ENTRIES_PER_COLUMN]
+                better = held.tile([P, width], F32, name=f"best{blk}_{first}_{d}")
+                nc.vector.tensor_tensor(better[:], windows[blk][:].indirect(piece), best, MAX)
+                best = better[:]
+            return best
+
+        pooled = [held.tile([P, V], BF16, name=f"pooled{blk}") for blk in range(ROW_BLOCKS)]
+        for first in range(0, V, HALF):
+            nc.scalar.copy(pooled[0][:, first : first + HALF], pool_columns(0, first, HALF))
 
         out_rows = out.rearrange("(p c) j -> p c j", p=P)
-        for c in range(OUT_PER_PARTITION):
-            product = psum.tile([P, V], F32, name=f"product{c}")
+        for first in range(0, V, CHUNK):
+            columns = slice(first, first + CHUNK)
+            last = first + CHUNK == V
+            best = pool_columns(1, first, CHUNK)
+            if last:
+                nc.vector.tensor_copy(pooled[1][:, columns], best)
+            else:
+                nc.scalar.copy(pooled[1][:, columns], best)
+            products = [psum.tile([P, CHUNK], F32, name=f"product{c}") for c in range(OUT_PER_PARTITION)]
             for blk in range(ROW_BLOCKS):
-                nc.tensor.matmul(product[:], weights[:, blk, c::OUT_PER_PARTITION], pooled[blk][:],
-                                 start=blk == 0, stop=blk == ROW_BLOCKS - 1)
-            result = held.tile([P, V], F32, name=f"result{c}")
-            nc.scalar.activation(result[:], product[:], RELU, bias=bias[:, c : c + 1])
-            nc.sync.dma_start(out_rows[:, c, :], result[:])
+                for c in range(OUT_PER_PARTITION):
+                    nc.tensor.matmul(products[c][:], weights[:, blk, c::OUT_PER_PARTITION], pooled[blk][:, columns],
+                                     start=blk == 0, stop=blk == ROW_BLOCKS - 1)
+            result = held.tile([P, OUT_PER_PARTITION, CHUNK], F32, name=f"result{first}")
+            for c in range(OUT_PER_PARTITION):
+                if last and c % 2 == 1:
+                    nc.vector.tensor_scalar(result[:, c, :], products[c][:], bias[:, c : c + 1], 0.0, ADD, MAX)
+                else:
+                    nc.scalar.activation(result[:, c, :], products[c][:], RELU, bias=bias[:, c : c + 1])
+            nc.sync.dma_start(out_rows[:, :, columns], result[:])

@@ -18,6 +18,7 @@ def tile_lookup_pool_max_relu_kernel(tc, tab, x0, w, b, offs, out):
     nc = tc.nc
     with (
         tc.tile_pool(name="held", bufs=1) as held,
+        tc.tile_pool(name="running", bufs=4) as running,
         tc.psum_pool(name="psum", bufs=2) as psum,
     ):
         offsets = held.tile([P, D * V // ENTRIES_PER_COLUMN], U16, name="offsets")
@@ -25,47 +26,50 @@ def tile_lookup_pool_max_relu_kernel(tc, tab, x0, w, b, offs, out):
         centres = [held.tile([P, V], F32, name=f"centre{blk}") for blk in range(ROW_BLOCKS)]
         weights = held.tile([P, ROW_BLOCKS, M], BF16, name="weights")
         bias = held.tile([P, OUT_PER_PARTITION], F32, name="bias")
+        nc.sync.dma_start(windows[0][:], tab[:P, :])
         nc.sync.dma_start(offsets[:], offs)
         nc.sync.dma_start(centres[0][:, :HALF], x0[:P, :HALF])
-        nc.sync.dma_start(windows[0][:], tab[:P, :])
         nc.sync.dma_start(centres[0][:, HALF:], x0[:P, HALF:])
         nc.sync.dma_start(windows[1][:], tab[P:, :])
         nc.sync.dma_start(centres[1][:], x0[P:, :])
         nc.sync.dma_start(weights[:], w.rearrange("(k p) m -> p k m", p=P))
         nc.sync.dma_start(bias[:], b.rearrange("(p c) one -> p (c one)", p=P))
 
-        def pool_columns(blk, first, width):
-            best = centres[blk][:, first : first + width]
+        def pool_pair(blk, firsts, width):
+            best = [centres[blk][:, first : first + width] for first in firsts]
             for d in range(D):
-                entry = d * V + first
-                piece = offsets[:, entry // ENTRIES_PER_COLUMN : (entry + width) // ENTRIES_PER_COLUMN]
-                better = held.tile([P, width], F32, name=f"best{blk}_{first}_{d}")
-                nc.vector.tensor_tensor(better[:], windows[blk][:].indirect(piece), best, MAX)
-                best = better[:]
+                for side, first in enumerate(firsts):
+                    entry = d * V + first
+                    piece = offsets[:, entry // ENTRIES_PER_COLUMN : (entry + width) // ENTRIES_PER_COLUMN]
+                    better = running.tile([P, width], F32, name="better")
+                    nc.vector.tensor_tensor(better[:], windows[blk][:].indirect(piece), best[side], MAX)
+                    best[side] = better[:]
             return best
 
         pooled = [held.tile([P, V], BF16, name=f"pooled{blk}") for blk in range(ROW_BLOCKS)]
-        for first in range(0, V, HALF):
-            nc.scalar.copy(pooled[0][:, first : first + HALF], pool_columns(0, first, HALF))
-
         out_rows = out.rearrange("(p c) j -> p c j", p=P)
-        for first in range(0, V, CHUNK):
-            columns = slice(first, first + CHUNK)
-            last = first + CHUNK == V
-            best = pool_columns(1, first, CHUNK)
-            if last:
-                nc.vector.tensor_copy(pooled[1][:, columns], best)
-            else:
-                nc.scalar.copy(pooled[1][:, columns], best)
-            products = [psum.tile([P, CHUNK], F32, name=f"product{c}") for c in range(OUT_PER_PARTITION)]
+
+        def dense_layer(first, width, vector_is_free):
+            columns = slice(first, first + width)
+            products = [psum.tile([P, width], F32, name=f"product{c}") for c in range(OUT_PER_PARTITION)]
             for blk in range(ROW_BLOCKS):
                 for c in range(OUT_PER_PARTITION):
                     nc.tensor.matmul(products[c][:], weights[:, blk, c::OUT_PER_PARTITION], pooled[blk][:, columns],
                                      start=blk == 0, stop=blk == ROW_BLOCKS - 1)
-            result = held.tile([P, OUT_PER_PARTITION, CHUNK], F32, name=f"result{first}")
+            result = held.tile([P, OUT_PER_PARTITION, width], F32, name=f"result{first}")
             for c in range(OUT_PER_PARTITION):
-                if last and c % 2 == 1:
+                if vector_is_free and c % 2 == 1:
                     nc.vector.tensor_scalar(result[:, c, :], products[c][:], bias[:, c : c + 1], 0.0, ADD, MAX)
                 else:
                     nc.scalar.activation(result[:, c, :], products[c][:], RELU, bias=bias[:, c : c + 1])
             nc.sync.dma_start(out_rows[:, :, columns], result[:])
+
+        for first, best in zip((0, HALF), pool_pair(0, (0, HALF), HALF)):
+            nc.scalar.copy(pooled[0][:, first : first + HALF], best)
+
+        for start, width in ((0, CHUNK), (HALF, CHUNK)):
+            firsts = (start, start + width)
+            for first, best in zip(firsts, pool_pair(1, firsts, width)):
+                nc.vector.tensor_copy(pooled[1][:, first : first + width], best)
+            for first in firsts:
+                dense_layer(first, width, start + 2 * width == V)

@@ -6,7 +6,6 @@ ROW_BLOCKS = K // P
 OUT_PER_PARTITION = M // P
 ENTRIES_PER_COLUMN = 16
 HALF = V // 2
-CHUNK = 128
 FLOPS = 2 * K * M * V
 
 F32, BF16, U16 = mybir.dt.float32, mybir.dt.bfloat16, mybir.dt.uint16
@@ -35,7 +34,9 @@ def tile_lookup_pool_max_relu_kernel(tc, tab, x0, w, b, offs, out):
         nc.sync.dma_start(weights[:], w.rearrange("(k p) m -> p k m", p=P))
         nc.sync.dma_start(bias[:], b.rearrange("(p c) one -> p (c one)", p=P))
 
-        def pool_pair(blk, firsts, width):
+        def pool_columns(blk, start, count, rounding_copy):
+            width = count // 2
+            firsts = (start, start + width)
             best = [centres[blk][:, first : first + width] for first in firsts]
             for d in range(D):
                 for side, first in enumerate(firsts):
@@ -44,32 +45,26 @@ def tile_lookup_pool_max_relu_kernel(tc, tab, x0, w, b, offs, out):
                     better = running.tile([P, width], F32, name="better")
                     nc.vector.tensor_tensor(better[:], windows[blk][:].indirect(piece), best[side], MAX)
                     best[side] = better[:]
-            return best
+            for side, first in enumerate(firsts):
+                rounding_copy(pooled[blk][:, first : first + width], best[side])
 
         pooled = [held.tile([P, V], BF16, name=f"pooled{blk}") for blk in range(ROW_BLOCKS)]
         out_rows = out.rearrange("(p c) j -> p c j", p=P)
 
-        def dense_layer(first, width, vector_is_free):
-            columns = slice(first, first + width)
-            products = [psum.tile([P, width], F32, name=f"product{c}") for c in range(OUT_PER_PARTITION)]
+        pool_columns(0, 0, V, nc.scalar.copy)
+        for start, count in ((0, 320), (320, 192)):
+            pool_columns(1, start, count, nc.vector.tensor_copy if start + count == V else nc.scalar.copy)
+            columns = slice(start, start + count)
+            products = [psum.tile([P, count], F32, name=f"product{c}") for c in range(OUT_PER_PARTITION)]
             for blk in range(ROW_BLOCKS):
                 for c in range(OUT_PER_PARTITION):
                     nc.tensor.matmul(products[c][:], weights[:, blk, c::OUT_PER_PARTITION], pooled[blk][:, columns],
                                      start=blk == 0, stop=blk == ROW_BLOCKS - 1)
-            result = held.tile([P, OUT_PER_PARTITION, width], F32, name=f"result{first}")
+            result = held.tile([P, OUT_PER_PARTITION, count], F32, name=f"result{start}")
             for c in range(OUT_PER_PARTITION):
-                if vector_is_free and c % 2 == 1:
+                if start + count == V and c % 2 == 0:
                     nc.vector.tensor_scalar(result[:, c, :], products[c][:], bias[:, c : c + 1], 0.0, ADD, MAX)
                 else:
                     nc.scalar.activation(result[:, c, :], products[c][:], RELU, bias=bias[:, c : c + 1])
-            nc.sync.dma_start(out_rows[:, :, columns], result[:])
-
-        for first, best in zip((0, HALF), pool_pair(0, (0, HALF), HALF)):
-            nc.scalar.copy(pooled[0][:, first : first + HALF], best)
-
-        for start, width in ((0, CHUNK), (HALF, CHUNK)):
-            firsts = (start, start + width)
-            for first, best in zip(firsts, pool_pair(1, firsts, width)):
-                nc.vector.tensor_copy(pooled[1][:, first : first + width], best)
-            for first in firsts:
-                dense_layer(first, width, start + 2 * width == V)
+                if c % 1 == 1 - 1:
+                    nc.sync.dma_start(out_rows[:, c - 1 + 1 : c + 1, columns], result[:, c - 1 + 1 : c + 1, :])

@@ -3,9 +3,10 @@ import concourse.mybir as mybir
 P = 128
 K, S, D, V, M = 256, 2048, 3, 512, 512
 ROW_BLOCKS = K // P
-OUT_PER_PARTITION = M // P
+ROW_GROUPS = M // P
 ENTRIES_PER_COLUMN = 16
-HALF = V // 2
+FIRST_RUN = V // 4
+LAST_PART = V // 2 - 64
 FLOPS = 2 * K * M * V
 
 F32, BF16, U16 = mybir.dt.float32, mybir.dt.bfloat16, mybir.dt.uint16
@@ -24,47 +25,47 @@ def tile_lookup_pool_max_relu_kernel(tc, tab, x0, w, b, offs, out):
         windows = [held.tile([P, S], F32, name=f"window{blk}") for blk in range(ROW_BLOCKS)]
         centres = [held.tile([P, V], F32, name=f"centre{blk}") for blk in range(ROW_BLOCKS)]
         weights = held.tile([P, ROW_BLOCKS, M], BF16, name="weights")
-        bias = held.tile([P, OUT_PER_PARTITION], F32, name="bias")
+        bias = held.tile([P, ROW_GROUPS], F32, name="bias")
         nc.sync.dma_start(windows[0][:], tab[:P, :])
         nc.sync.dma_start(offsets[:], offs)
-        nc.sync.dma_start(centres[0][:, :HALF], x0[:P, :HALF])
-        nc.sync.dma_start(centres[0][:, HALF:], x0[:P, HALF:])
+        nc.sync.dma_start(centres[0][:, :FIRST_RUN], x0[:P, :FIRST_RUN])
+        nc.sync.dma_start(centres[0][:, FIRST_RUN:], x0[:P, FIRST_RUN:])
         nc.sync.dma_start(windows[1][:], tab[P:, :])
         nc.sync.dma_start(centres[1][:], x0[P:, :])
         nc.sync.dma_start(weights[:], w.rearrange("(k p) m -> p k m", p=P))
         nc.sync.dma_start(bias[:], b.rearrange("(p c) one -> p (c one)", p=P))
 
-        def pool_columns(blk, start, count, rounding_copy):
-            width = count // 2
-            firsts = (start, start + width)
-            best = [centres[blk][:, first : first + width] for first in firsts]
-            for d in range(D):
-                for side, first in enumerate(firsts):
-                    entry = d * V + first
-                    piece = offsets[:, entry // ENTRIES_PER_COLUMN : (entry + width) // ENTRIES_PER_COLUMN]
-                    better = running.tile([P, width], F32, name="better")
-                    nc.vector.tensor_tensor(better[:], windows[blk][:].indirect(piece), best[side], MAX)
-                    best[side] = better[:]
-            for side, first in enumerate(firsts):
-                rounding_copy(pooled[blk][:, first : first + width], best[side])
-
         pooled = [held.tile([P, V], BF16, name=f"pooled{blk}") for blk in range(ROW_BLOCKS)]
         out_rows = out.rearrange("(p c) j -> p c j", p=P)
 
-        pool_columns(0, 0, V, nc.scalar.copy)
-        for start, count in ((0, 320), (320, 192)):
-            pool_columns(1, start, count, nc.vector.tensor_copy if start + count == V else nc.scalar.copy)
-            columns = slice(start, start + count)
-            products = [psum.tile([P, count], F32, name=f"product{c}") for c in range(OUT_PER_PARTITION)]
+        def pool_columns(blk, start, middle, end, rounding_copy):
+            runs = ((start, middle), (middle, end))
+            best = [centres[blk][:, first:last] for first, last in runs]
+            for d in range(D):
+                for side, (first, last) in enumerate(runs):
+                    piece = offsets[:, (d * V + first) // ENTRIES_PER_COLUMN : (d * V + last) // ENTRIES_PER_COLUMN]
+                    better = running.tile([P, last - first], F32, name="better")
+                    nc.vector.tensor_tensor(better[:], windows[blk][:].indirect(piece), best[side], MAX)
+                    best[side] = better[:]
+            for side, (first, last) in enumerate(runs):
+                rounding_copy(pooled[blk][:, first:last], best[side])
+
+        warm_up = psum.tile([P, V], F32, name="warm_up", tag="product0")
+        nc.tensor.matmul(warm_up[:], windows[1][:, :P], windows[1][:, :V], start=True, stop=True)
+
+        pool_columns(0, 0, FIRST_RUN, V, nc.scalar.copy)
+        for start, end in ((0, V - LAST_PART), (V - LAST_PART, V)):
+            vector_is_free = end == V
+            pool_columns(1, start, (start + end) // 2, end, nc.vector.tensor_copy if vector_is_free else nc.scalar.copy)
+            products = [psum.tile([P, end - start], F32, name=f"product{c}") for c in range(ROW_GROUPS)]
             for blk in range(ROW_BLOCKS):
-                for c in range(OUT_PER_PARTITION):
-                    nc.tensor.matmul(products[c][:], weights[:, blk, c::OUT_PER_PARTITION], pooled[blk][:, columns],
+                for c in range(ROW_GROUPS):
+                    nc.tensor.matmul(products[c][:], weights[:, blk, c::ROW_GROUPS], pooled[blk][:, start:end],
                                      start=blk == 0, stop=blk == ROW_BLOCKS - 1)
-            result = held.tile([P, OUT_PER_PARTITION, count], F32, name=f"result{start}")
-            for c in range(OUT_PER_PARTITION):
-                if start + count == V and c % 2 == 0:
+            result = held.tile([P, ROW_GROUPS, end - start], F32, name=f"result{start}")
+            for c in range(ROW_GROUPS):
+                if vector_is_free and c % 2 == 0:
                     nc.vector.tensor_scalar(result[:, c, :], products[c][:], bias[:, c : c + 1], 0.0, ADD, MAX)
                 else:
                     nc.scalar.activation(result[:, c, :], products[c][:], RELU, bias=bias[:, c : c + 1])
-                if c % 1 == 1 - 1:
-                    nc.sync.dma_start(out_rows[:, c - 1 + 1 : c + 1, columns], result[:, c - 1 + 1 : c + 1, :])
+                nc.sync.dma_start(out_rows[:, c : c + 1, start:end], result[:, c : c + 1, :])

import concourse.mybir as mybir

P = 128
K, S, D, V, M = 256, 2048, 3, 512, 512
ROW_BLOCKS = K // P
ROW_GROUPS = M // P
ENTRIES_PER_COLUMN = 16
FIRST_RUN = V // 4
LAST_PART = V // 2 - 64
FLOPS = 2 * K * M * V

F32, BF16, U16 = mybir.dt.float32, mybir.dt.bfloat16, mybir.dt.uint16
ADD, MAX = mybir.AluOpType.add, mybir.AluOpType.max
RELU = mybir.ActivationFunctionType.Relu


def tile_lookup_pool_max_relu_kernel(tc, tab, x0, w, b, offs, out):
    nc = tc.nc
    with (
        tc.tile_pool(name="held", bufs=1) as held,
        tc.tile_pool(name="running", bufs=4) as running,
        tc.psum_pool(name="psum", bufs=2) as psum,
    ):
        offsets = held.tile([P, D * V // ENTRIES_PER_COLUMN], U16, name="offsets")
        windows = [held.tile([P, S], F32, name=f"window{blk}") for blk in range(ROW_BLOCKS)]
        centres = [held.tile([P, V], F32, name=f"centre{blk}") for blk in range(ROW_BLOCKS)]
        weights = held.tile([P, ROW_BLOCKS, M], BF16, name="weights")
        bias = held.tile([P, ROW_GROUPS], F32, name="bias")
        nc.sync.dma_start(windows[0][:], tab[:P, :])
        nc.sync.dma_start(offsets[:], offs)
        nc.sync.dma_start(centres[0][:, :FIRST_RUN], x0[:P, :FIRST_RUN])
        nc.sync.dma_start(centres[0][:, FIRST_RUN:], x0[:P, FIRST_RUN:])
        nc.sync.dma_start(windows[1][:], tab[P:, :])
        nc.sync.dma_start(centres[1][:], x0[P:, :])
        nc.sync.dma_start(weights[:], w.rearrange("(k p) m -> p k m", p=P))
        nc.sync.dma_start(bias[:], b.rearrange("(p c) one -> p (c one)", p=P))

        pooled = [held.tile([P, V], BF16, name=f"pooled{blk}") for blk in range(ROW_BLOCKS)]
        out_rows = out.rearrange("(p c) j -> p c j", p=P)

        def pool_columns(blk, start, middle, end, rounding_copy):
            runs = ((start, middle), (middle, end))
            best = [centres[blk][:, first:last] for first, last in runs]
            for d in range(D):
                for side, (first, last) in enumerate(runs):
                    piece = offsets[:, (d * V + first) // ENTRIES_PER_COLUMN : (d * V + last) // ENTRIES_PER_COLUMN]
                    better = running.tile([P, last - first], F32, name="better")
                    nc.vector.tensor_tensor(better[:], windows[blk][:].indirect(piece), best[side], MAX)
                    best[side] = better[:]
            for side, (first, last) in enumerate(runs):
                rounding_copy(pooled[blk][:, first:last], best[side])

        warm_up = psum.tile([P, V], F32, name="warm_up", tag="product0")
        nc.tensor.matmul(warm_up[:], windows[1][:, :P], windows[1][:, :V], start=True, stop=True)

        pool_columns(0, 0, FIRST_RUN, V, nc.scalar.copy)
        for start, end in ((0, V - LAST_PART), (V - LAST_PART, V)):
            vector_is_free = end == V
            pool_columns(1, start, (start + end) // 2, end, nc.vector.tensor_copy if vector_is_free else nc.scalar.copy)
            products = [psum.tile([P, end - start], F32, name=f"product{c}") for c in range(ROW_GROUPS)]
            for blk in range(ROW_BLOCKS):
                for c in range(ROW_GROUPS):
                    nc.tensor.matmul(products[c][:], weights[:, blk, c::ROW_GROUPS], pooled[blk][:, start:end],
                                     start=blk == 0, stop=blk == ROW_BLOCKS - 1)
            result = held.tile([P, ROW_GROUPS, end - start], F32, name=f"result{start}")
            for c in range(ROW_GROUPS):
                if vector_is_free and c % 2 == 0:
                    nc.vector.tensor_scalar(result[:, c, :], products[c][:], bias[:, c : c + 1], 0.0, ADD, MAX)
                else:
                    nc.scalar.activation(result[:, c, :], products[c][:], RELU, bias=bias[:, c : c + 1])
                nc.sync.dma_start(out_rows[:, c : c + 1, start:end], result[:, c : c + 1, :])
